import numpy as np, ml_dtypes
CORES = [35,38,43,46]
N = 4
import mx_ref
BF = ml_dtypes.bfloat16
def entries(a):
    return np.ascontiguousarray(a.T).reshape(-1)
def table(e):
    return np.ascontiguousarray(np.reshape(e, (-1, 16)).T).astype(np.int32)
def cols(t, e):
    v = np.concatenate([t.reshape(128, -1, 4), np.zeros((128, 1, 4), BF)], axis=1)
    return np.ascontiguousarray(v[:, e]).reshape(128, -1)
def tile(rs):
    return np.stack(rs, axis=2).reshape(128, -1).astype(BF)
def cut(t, i, w=512):
    return t[:, w * i:w * i + w]
def rowtile(v, k):
    z = np.concatenate([v, np.zeros((1, v.shape[1]), BF)])
    return np.concatenate([np.ascontiguousarray(z[k[:, 4 * m:4 * m + 4]].transpose(0, 2, 1)).reshape(128, -1) for m in range(k.shape[1] // 4)], axis=1)
def f(rng, *shape):
    return mx_ref.flush((rng.standard_normal(shape, dtype=np.float32) * np.exp2(rng.integers(-2, 3, shape[:-1] + (1,)))).astype(BF))
def wide(rng, *shape, cols=0):
    v = rng.standard_normal(shape, dtype=np.float32) * np.exp2(rng.integers(-12, 13, shape)).astype(np.float32)
    if cols: v *= np.repeat(np.exp2(rng.integers(-cols, cols + 1, shape[:-2] + (1, shape[-1] // 4))) * (rng.random(shape[:-2] + (1, shape[-1] // 4)) > 0.0625), 4, axis=-1).astype(np.float32)
    return mx_ref.flush(v.astype(BF))
T, HU, ACT = 512, 1024, 512
def lists(rng, how=None):
    a = []
    for r in range(N):
        e = rng.permutation(HU)[:ACT]
        if how == "reversed": e = np.sort(e)[::-1]
        if how == "clustered": e = rng.integers(0, HU - ACT + 1) + np.arange(ACT)
        a.append(e)
    return {"act": np.stack([e.reshape(128, 4).astype(np.int32) for e in a]), "actc": np.stack([table(e) for e in a])}
def setup_inputs(rng):
    return {"x": f(rng, N, 128, 4 * T), "w1": f(rng, N, 128, 4 * HU), "w2": f(rng, N, HU, 512), **lists(rng)}
def setup_inputs_clustered(rng):
    return {**setup_inputs(rng), **lists(rng, "clustered")}
def setup_inputs_dead(rng):
    d = setup_inputs(rng); d["x"] = np.abs(d["x"])
    for r in range(N):
        k = d["act"][r].reshape(-1)[rng.permutation(ACT)[:ACT // 2]]
        w = d["w1"][r].reshape(128, HU, 4)
        w[:, k] = -np.abs(w[:, k])
        d["w1"][r] = w.reshape(128, -1)
    return d
def setup_inputs_giant(rng):
    d = setup_inputs(rng)
    for r in range(N):
        k = d["act"][r].reshape(-1)[rng.permutation(ACT)[:ACT // 32]]
        d["w2"][r, k] = (d["w2"][r, k].astype(np.float32) * np.float32(4096)).astype(BF)
    return d
def setup_inputs_reversed(rng):
    return {**setup_inputs(rng), **lists(rng, "reversed")}
def setup_inputs_spread(rng):
    d = setup_inputs(rng); d["x"] = wide(rng, N, 128, 4 * T); d["w2"] = wide(rng, N, HU, 512); return d
def check_inputs(d):
    b = []
    for r in range(N):
        e = d["act"][r].reshape(-1)
        if e.min() < 0 or e.max() >= HU or len(set(e.tolist())) != ACT: b.append("act")
        if (entries(d["actc"][r]) != e).any(): b.append("actc")
    return b
def reference(x, w1, w2, act, actc):
    y = np.zeros((N, 128, 4 * T), np.float32)
    X = [mx_ref.quantize(x[r]) for r in range(N)]
    for s in range(N):
        A = [mx_ref.quantize(cols(w1[s], act[s][:, b])) for b in range(4)]
        rows = rowtile(w2[s], act[s])
        B = [mx_ref.quantize(np.ascontiguousarray(cut(rows, o))) for o in range(4)]
        for r in range(N):
            H = mx_ref.quantize(tile([np.maximum(mx_ref.matmul(A[b], X[r]), np.float32(0)) * np.float32(0.05) for b in range(4)]))
            for o in range(4): y[r][:, T * o:T * o + T] += mx_ref.matmul(B[o], H)
    return {"y": y}

@@ -1,0 +1,220 @@
+from concourse.bass import DstId, RemoteDMATransfer, IndirectOffsetOnAxis
+from concourse.mybir import dt, AluOpType, ActivationFunctionType
+
+N, C = 4, 512
+W = 4 * C
+BF, F8 = "bfloat16", "float8_e4m3fn_x4"
+SCRATCH = {
+    "lst": ("sbuf", [128, 4], "int32"),
+    "tabs": ("sbuf", [128, 32], "int32"),
+    "quad": ("sbuf", [128, 32], "int32"),
+    "offs": ("sbuf", [128, 128], "uint16"),
+    "w1b": ("sbuf", [128, 4096], BF), "xb": ("sbuf", [128, W], BF), "ab": ("sbuf", [128, W], BF),
+    "w2g": ("sbuf", [128, W], BF), "bb": ("sbuf", [128, W], BF),
+    "h0": ("sbuf", [128, W], BF), "h1": ("sbuf", [128, W], BF), "h2": ("sbuf", [128, W], BF), "h3": ("sbuf", [128, W], BF),
+    "xq": ("sbuf", [128, C], F8), "xp": ("sbuf", [128, C], "uint8"),
+    "aq": ("sbuf", [128, N * C], F8), "ap": ("sbuf", [128, N * C], "uint8"),
+    "bq": ("sbuf", [128, N * C], F8), "bp": ("sbuf", [128, N * C], "uint8"),
+    "hq": ("sbuf", [128, N * C], F8), "hp": ("sbuf", [128, N * C], "uint8"),
+    "yb": ("sbuf", [128, W], "float32"),
+    "zps": ("psum", [128, W], "float32"),
+    "yps": ("psum", [128, W], "float32"),
+}
+SEMAPHORES = (["lact", "ltab", "lw1", "lx", "lxg", "vquad", "vrep", "voff", "gath0", "gath1", "qa0", "qa1", "qx", "qb",
+               "bcs", "bcv", "sent", "stored"]
+              + ["%s%d" % (k, i) for i in range(4) for k in ("ix", "z", "e", "h", "yd", "yc", "ax", "ay", "az", "bx", "by", "bz")])
+
+
+def lanes(core, cores, topo):
+    others = [c for c in cores if c != core]
+    far = [c for c in others if topo.chip(c) != topo.chip(core)]
+    near = [c for c in others if topo.chip(c) == topo.chip(core)]
+    out = sorted({e for c in far for e in topo.engines(core, c)})
+    plan = {}
+    for group, es in ((far, out), (near, [e for c in near[:1] for e in topo.engines(core, c) if e not in out])):
+        for i, c in enumerate(group):
+            k = len(es) // len(group)
+            plan[c] = es[i * k:i * k + k]
+    return plan
+
+
+def rank_program(g, core, T, topo):
+    r = T.rank_of(core)
+    if r is None:
+        return
+    S = T.sem
+    MUL, ADD, MAX = AluOpType.mult, AluOpType.add, AluOpType.max
+    COPY, RELU = ActivationFunctionType.Copy, ActivationFunctionType.Relu
+    cores = list(T.cores)
+    send = lanes(core, cores, topo)
+    recv = {s: lanes(cores[s], cores, topo)[core] for s in range(N) if s != r}
+    near = [s for s in recv if topo.chip(cores[s]) == topo.chip(core)]
+    far = sorted([s for s in recv if s not in near], key=lambda s: topo.die(cores[s]) != topo.die(core))
+    order = [r] + near + far
+
+    def q(name, s, a=0, n=C):
+        return T[name][:, C * s + a:C * s + a + n]
+
+    def tab(eng, h, c):
+        eng.dma_start(T.tabs[16 * h:16 * h + 16, 4 * c:4 * c + 4], T.act[16 * c:16 * c + 16, :]).then_inc(S.ltab, 16)
+
+    XG = 256
+    g.sync.dma_start(T.lst[:], T.act[:]).then_inc(S.lact, 16)
+    for c in range(8):
+        tab(g.sync, 0, c)
+        tab(g.scalar, 1, c)
+    g.scalar.dma_start(T.w1b[:], T.w1[:]).then_inc(S.lw1, 16)
+    g.scalar.dma_start(T.xb[:, XG:], T.x[:, XG:]).then_inc(S.lx, 16)
+    g.dma_start(T.xb[:, 0:XG], T.x[:, 0:XG]).then_inc(S.lxg, 16)
+
+    total = [0]
+
+    def fused(sem, pieces):
+        tr = []
+        for c in cores:
+            if c == core:
+                continue
+            rid, pid, _ = topo.addr(c)
+            n = len(send[c]) // len(pieces)
+            for i, p in enumerate(pieces):
+                tr.append(RemoteDMATransfer(dst_ids=[DstId(rid=rid, pnc=pid)], dma_engine_mask=sum(1 << e for e in send[c][i * n:i * n + n]),
+                                            remote_sem=S["%s%d" % (sem, r)], src=p, dst=p))
+                total[0] += n
+        g.remote_dma_fused(tr, local_sem=S.sent)
+
+    def codes(name, b, n=1):
+        return q(name, r, 128 * b, 128 * n).bitcast(dt.uint8)
+
+    g.wait_ge(S.lact, 16)
+    for t in range(4):
+        if t == 3:
+            g.wait_ge(S.qa0, 1)
+            fused("ax", [codes("aq", 0, 2)])
+        g.indirect_dma_start(T.w2g[:, C * t:C * t + C], None, T.w2[:], IndirectOffsetOnAxis(ap=T.lst[:, t:t + 1], axis=0),
+                             bounds_check=1023).then_inc(S["ix%d" % t], 16)
+    g.wait_ge(S.qa1, 1)
+    fused("ay", [q("ap", r), codes("aq", 2)])
+    fused("az", [codes("aq", 3)])
+    g.wait_ge(S.qb, 1)
+    fused("bx", [q("bp", r), codes("bq", 0)])
+    fused("by", [codes("bq", 1), codes("bq", 2)])
+    fused("bz", [codes("bq", 3)])
+    g.wait_ge(S.sent, total[0])
+
+    v, a = g.vector, g.scalar
+    v.wait_ge(S.ltab, 256)
+    for b in range(4):
+        v.tensor_scalar(T.quad[0:32, 8 * b:8 * b + 8], T.tabs[0:32, b:32:4], 4, None, MUL).then_inc(S.vquad, 1)
+    v.wait_ge(S.vquad, 4)
+    for k in range(1, 4):
+        v.tensor_copy(T.quad[32 * k:32 * k + 32, :], T.quad[0:32, :]).then_inc(S.vrep, 1)
+    v.wait_ge(S.vrep, 3)
+    for t in range(4):
+        v.tensor_scalar(T.offs[:, 32 * t:32 * t + 32], T.quad[:], t, None, ADD).then_inc(S.voff, 1)
+    for e in (v, a):
+        e.wait_ge(S.voff, 4)
+        e.wait_ge(S.lw1, 16)
+    for k, (lo, hi) in enumerate(((0, 256), (256, 512))):
+
+        def gather(t):
+            return (T.ab[:, 4 * lo + t:4 * hi:4],
+                    T.w1b[:, 0:4096].indirect(T.offs[:, 32 * t + lo // 16:32 * t + hi // 16]))
+
+        for t in (0, 1):
+            v.tensor_copy(*gather(t)).then_inc(S["gath%d" % k], 1)
+        for t in (2, 3):
+            a.activation(*gather(t), COPY).then_inc(S["gath%d" % k], 1)
+        v.wait_ge(S["gath%d" % k], 4)
+        v.quantize_mx(q("aq", r, lo, hi - lo), q("ap", r, lo, hi - lo), T.ab[:, 4 * lo:4 * hi]).then_inc(S["qa%d" % k], 1)
+    v.wait_ge(S.lx, 16)
+    v.wait_ge(S.lxg, 16)
+    v.quantize_mx(T.xq[:], T.xp[:], T.xb[:]).then_inc(S.qx, 1)
+
+    def relu(i, b, vec):
+        e = v if vec else a
+        out, z = T["h%d" % order[i]][:, b:W:4], T.zps[:, C * b:C * b + C]
+        e.wait_ge(S["z%d" % b], i + 1)
+        if vec:
+            v.tensor_scalar(out, z, 0.0, 0.05, MAX, MUL).then_inc(S["e%d" % b], 1)
+        else:
+            a.activation(out, z, RELU, scale=0.05).then_inc(S["e%d" % b], 1)
+
+    def hidden(i, scal, vect):
+        s = order[i]
+        for b in scal:
+            relu(i, b, False)
+        for b in vect:
+            relu(i, b, True)
+        for b in range(4):
+            v.wait_ge(S["e%d" % b], i + 1)
+        v.quantize_mx(q("hq", s), q("hp", s), T["h%d" % s][:]).then_inc(S["h%d" % s], 1)
+
+    def rows(t):
+        return T.bb[:, t:W:4], T.w2g[:, C * t:C * t + C]
+
+    for t in (0, 1):
+        a.wait_ge(S["ix%d" % t], 16)
+        a.activation(*rows(t), COPY).then_inc(S.bcs, 1)
+    hidden(0, (0, 2), (1, 3))
+    a.wait_ge(S.ix2, 16)
+    a.activation(*rows(2), COPY).then_inc(S.bcs, 1)
+    v.wait_ge(S.ix3, 16)
+    v.tensor_copy(*rows(3)).then_inc(S.bcv, 1)
+    v.wait_ge(S.bcv, 1)
+    v.wait_ge(S.bcs, 3)
+    v.quantize_mx(q("bq", r), q("bp", r), T.bb[:]).then_inc(S.qb, 1)
+    hidden(1, (0, 1, 2), (3,))
+    hidden(2, (0, 2), (1, 3))
+    hidden(3, (0, 1, 2), (3,))
+    for o in range(4):
+        cols = slice(C * o, C * o + C)
+        (a if o % 2 else v).wait_ge(S["yd%d" % o], 1)
+        if o % 2 == 0:
+            v.tensor_copy(T.yb[:, cols], T.yps[:, cols]).then_inc(S["yc%d" % o], 1)
+        else:
+            a.activation(T.yb[:, cols], T.yps[:, cols], COPY).then_inc(S["yc%d" % o], 1)
+
+    p = g.tensor
+
+    def first(i):
+        s = order[i]
+        for k in ("qa0", "qa1", "qx") if s == r else ():
+            p.wait_ge(S[k], 1)
+        for k in ("ax", "ay") if s != r else ():
+            p.wait_ge(S["%s%d" % (k, s)], len(recv[s]))
+        for b in range(4):
+            if s != r and b == 3:
+                p.wait_ge(S["az%d" % s], len(recv[s]))
+            if i:
+                p.wait_ge(S["e%d" % b], i)
+            p.matmul_mx(T.zps[:, C * b:C * b + C], q("aq", s, 128 * b, 128), q("ap", s, 128 * b, 128), T.xq[:], T.xp[:],
+                        True, True).then_inc(S["z%d" % b], 1)
+
+    def second(i, o):
+        s = order[i]
+        if o == 0:
+            p.wait_ge(S["h%d" % s], 1)
+        if s == r:
+            if o == 0:
+                p.wait_ge(S.qb, 1)
+        elif o != 2:
+            p.wait_ge(S["%s%d" % (("bx", "by", None, "bz")[o], s)], len(recv[s]))
+        m = p.matmul_mx(T.yps[:, C * o:C * o + C], q("bq", s, 128 * o, 128), q("bp", s, 128 * o, 128), q("hq", s), q("hp", s),
+                        i == 0, i == N - 1)
+        if i == N - 1:
+            m.then_inc(S["yd%d" % o], 1)
+
+    first(0)
+    first(1)
+    first(2)
+    second(0, 0)
+    second(0, 1)
+    first(3)
+    for i, o in ((0, 2), (0, 3), (1, 0), (2, 0), (1, 1), (1, 2), (1, 3), (3, 0), (2, 1), (3, 1), (2, 2), (3, 2), (2, 3), (3, 3)):
+        second(i, o)
+
+    for o in range(4):
+        cols = slice(C * o, C * o + C)
+        g.sync.wait_ge(S["yc%d" % o], 1)
+        g.sync.dma_start(T.y[:, cols], T.yb[:, cols]).then_inc(S.stored, 16)
+    g.sync.wait_ge(S.stored, 64)

@@ -6,8 +6,10 @@ W = 4 * C
 BF, F8 = "bfloat16", "float8_e4m3fn_x4"
 SCRATCH = {
     "lst": ("sbuf", [128, 4], "int32"),
-    "tabs": ("sbuf", [128, 32], "int32"),
-    "quad": ("sbuf", [128, 32], "int32"),
+    "tab0": ("sbuf", [128, 16], "int32"),
+    "tab1": ("sbuf", [128, 32], "float32"),
+    "tab2": ("sbuf", [128, 128], "float32"),
+    "tab3": ("sbuf", [128, 128], "float32"),
     "offs": ("sbuf", [128, 128], "uint16"),
     "w1b": ("sbuf", [128, 4096], BF), "xb": ("sbuf", [128, W], BF), "ab": ("sbuf", [128, W], BF),
     "w2g": ("sbuf", [128, W], BF), "bb": ("sbuf", [128, W], BF),
@@ -20,21 +22,40 @@ SCRATCH = {
     "zps": ("psum", [128, W], "float32"),
     "yps": ("psum", [128, W], "float32"),
 }
-SEMAPHORES = (["lact", "ltab", "lw1", "lx", "lxg", "vquad", "vrep", "voff", "gath0", "gath1", "qa0", "qa1", "qx", "qb",
-               "bcs", "bcv", "sent", "stored"]
-              + ["%s%d" % (k, i) for i in range(4) for k in ("ix", "z", "e", "h", "yd", "yc", "ax", "ay", "az", "bx", "by", "bz")])
+
+NEAR, FAR, OVER, PASS = 1, 2, 3, 4
+A_CALLS = [(2, {NEAR: ["01"], FAR: ["01"]}),
+           (3, {NEAR: ["P"], FAR: ["P"]}),
+           (3, {NEAR: ["23"], FAR: ["23"]}),
+           (4, {PASS: ["P"]}),
+           (4, {PASS: ["0123"]})]
+B_CALLS = [{k: [p] for k in (NEAR, FAR, OVER)} for p in ("0", "P", "12", "3")]
+
+SEMAPHORES = (["lact", "ltab", "lw1", "lx", "lxg", "vt1", "vt2", "vt3", "voff", "gath0", "gath1", "qa0", "qa1", "qx", "qb",
+               "qb0", "bcs", "bcv", "bcw", "sent", "stored", "yd4", "yc4"]
+              + ["%s%d" % (k, i) for i in range(4) for k in ("ix", "z", "e", "h", "yd", "yc")]
+              + ["a%d_%d" % (j, s) for j in range(len(A_CALLS)) for s in range(N)]
+              + ["b%d_%d" % (j, s) for j in range(len(B_CALLS)) for s in range(N)])
 
 
-def lanes(core, cores, topo):
-    others = [c for c in cores if c != core]
-    far = [c for c in others if topo.chip(c) != topo.chip(core)]
-    near = [c for c in others if topo.chip(c) == topo.chip(core)]
-    out = sorted({e for c in far for e in topo.engines(core, c)})
+def others(core, cores, topo):
+    def kind(c):
+        return 0 if c == core else NEAR if topo.chip(c) == topo.chip(core) else FAR if topo.die(c) == topo.die(core) else OVER
+    return sorted(range(N), key=lambda s: kind(cores[s]))
+
+
+def lanes(call, core, cores, topo):
+    order = others(core, cores, topo)
+    off = [(k, p) for k in (FAR, OVER) for p in call.get(k, [])]
+    on = [(k, p) for k in (NEAR, PASS) for p in call.get(k, [])]
+    out = topo.engines(core, cores[order[FAR]]) if off else []
     plan = {}
-    for group, es in ((far, out), (near, [e for c in near[:1] for e in topo.engines(core, c) if e not in out])):
-        for i, c in enumerate(group):
-            k = len(es) // len(group)
-            plan[c] = es[i * k:i * k + k]
+    for group, es in ((off, out), (on, [e for e in topo.engines(core, cores[order[NEAR]]) if e not in out])):
+        n = [1] * len(group)
+        while group and sum(n) + min(n) <= len(es):
+            n[n.index(min(n))] *= 2
+        for i, (k, p) in enumerate(group):
+            plan.setdefault(k, []).append((p, es[sum(n[:i]):sum(n[:i + 1])]))
     return plan
 
 
@@ -46,85 +67,85 @@ def rank_program(g, core, T, topo):
     MUL, ADD, MAX = AluOpType.mult, AluOpType.add, AluOpType.max
     COPY, RELU = ActivationFunctionType.Copy, ActivationFunctionType.Relu
     cores = list(T.cores)
-    send = lanes(core, cores, topo)
-    recv = {s: lanes(cores[s], cores, topo)[core] for s in range(N) if s != r}
-    near = [s for s in recv if topo.chip(cores[s]) == topo.chip(core)]
-    far = sorted([s for s in recv if s not in near], key=lambda s: topo.die(cores[s]) != topo.die(core))
-    order = [r] + near + far
+    order = others(core, cores, topo)
+    calls = {"a": [c for _, c in A_CALLS], "b": B_CALLS}
 
     def q(name, s, a=0, n=C):
         return T[name][:, C * s + a:C * s + a + n]
 
-    def tab(eng, h, c):
-        eng.dma_start(T.tabs[16 * h:16 * h + 16, 4 * c:4 * c + 4], T.act[16 * c:16 * c + 16, :]).then_inc(S.ltab, 16)
+    def arrival(m, i, piece):
+        for j, call in enumerate(calls[m]):
+            for k, sender in ((i, order[i]), (PASS if i == OVER else None, order[NEAR])):
+                if any(piece in p for p in call.get(k, [])):
+                    return S["%s%d_%d" % (m, j, order[i])], sum(len(es) for _, es in lanes(call, cores[sender], cores, topo)[k])
+
+    parts = [(o, 0, C, T.yps[:, C * o:C * o + C]) for o in range(3)]
+    parts += [(3, 0, C // 2, T.yps[:, 3 * C:3 * C + C // 2]), (3, C // 2, C, T.zps[:, 0:C // 2])]
 
     XG = 256
     g.sync.dma_start(T.lst[:], T.act[:]).then_inc(S.lact, 16)
-    for c in range(8):
-        tab(g.sync, 0, c)
-        tab(g.scalar, 1, c)
+    g.scalar.dma_start(T.tab0[0:32, :], T.act[:]).then_inc(S.ltab, 16)
     g.scalar.dma_start(T.w1b[:], T.w1[:]).then_inc(S.lw1, 16)
     g.scalar.dma_start(T.xb[:, XG:], T.x[:, XG:]).then_inc(S.lx, 16)
     g.dma_start(T.xb[:, 0:XG], T.x[:, 0:XG]).then_inc(S.lxg, 16)
 
     total = [0]
 
-    def fused(sem, pieces):
+    def fused(m, j):
         tr = []
-        for c in cores:
-            if c == core:
-                continue
-            rid, pid, _ = topo.addr(c)
-            n = len(send[c]) // len(pieces)
-            for i, p in enumerate(pieces):
-                tr.append(RemoteDMATransfer(dst_ids=[DstId(rid=rid, pnc=pid)], dma_engine_mask=sum(1 << e for e in send[c][i * n:i * n + n]),
-                                            remote_sem=S["%s%d" % (sem, r)], src=p, dst=p))
-                total[0] += n
+        for k, pieces in lanes(calls[m][j], core, cores, topo).items():
+            s = order[FAR] if k == PASS else r
+            rid, pid, _ = topo.addr(cores[order[NEAR if k == PASS else k]])
+            for p, es in pieces:
+                if k == PASS:
+                    for piece in p:
+                        g.wait_ge(*arrival(m, FAR, piece))
+                ap = q(m + "p", s) if p == "P" else q(m + "q", s, 128 * int(p[0]), 128 * len(p)).bitcast(dt.uint8)
+                tr.append(RemoteDMATransfer(dst_ids=[DstId(rid=rid, pnc=pid)], dma_engine_mask=sum(1 << e for e in es),
+                                            remote_sem=S["%s%d_%d" % (m, j, s)], src=ap, dst=ap))
+                total[0] += len(es)
         g.remote_dma_fused(tr, local_sem=S.sent)
 
-    def codes(name, b, n=1):
-        return q(name, r, 128 * b, 128 * n).bitcast(dt.uint8)
-
     g.wait_ge(S.lact, 16)
-    for t in range(4):
-        if t == 3:
-            g.wait_ge(S.qa0, 1)
-            fused("ax", [codes("aq", 0, 2)])
-        g.indirect_dma_start(T.w2g[:, C * t:C * t + C], None, T.w2[:], IndirectOffsetOnAxis(ap=T.lst[:, t:t + 1], axis=0),
-                             bounds_check=1023).then_inc(S["ix%d" % t], 16)
-    g.wait_ge(S.qa1, 1)
-    fused("ay", [q("ap", r), codes("aq", 2)])
-    fused("az", [codes("aq", 3)])
-    g.wait_ge(S.qb, 1)
-    fused("bx", [q("bp", r), codes("bq", 0)])
-    fused("by", [codes("bq", 1), codes("bq", 2)])
-    fused("bz", [codes("bq", 3)])
+    for t in range(5):
+        for j, (ahead, call) in enumerate(A_CALLS):
+            if ahead == t:
+                g.wait_ge(S.qa0, 1)
+                if j:
+                    g.wait_ge(S.qa1, 1)
+                fused("a", j)
+        if t < 4:
+            g.indirect_dma_start(T.w2g[:, C * t:C * t + C], None, T.w2[:], IndirectOffsetOnAxis(ap=T.lst[:, t:t + 1], axis=0),
+                                 bounds_check=1023).then_inc(S["ix%d" % t], 16)
+    for j in range(len(B_CALLS)):
+        if j < 2:
+            g.wait_ge((S.qb0, S.qb)[j], 1)
+        fused("b", j)
     g.wait_ge(S.sent, total[0])
 
     v, a = g.vector, g.scalar
-    v.wait_ge(S.ltab, 256)
-    for b in range(4):
-        v.tensor_scalar(T.quad[0:32, 8 * b:8 * b + 8], T.tabs[0:32, b:32:4], 4, None, MUL).then_inc(S.vquad, 1)
-    v.wait_ge(S.vquad, 4)
-    for k in range(1, 4):
-        v.tensor_copy(T.quad[32 * k:32 * k + 32, :], T.quad[0:32, :]).then_inc(S.vrep, 1)
-    v.wait_ge(S.vrep, 3)
+    v.wait_ge(S.ltab, 16)
+    for k in range(8):
+        v.tensor_copy(T.tab1[0:32, 4 * k:4 * k + 4], T.tab0[0:32, k // 2:16:4]).then_inc(S.vt1, 1)
+    v.wait_ge(S.vt1, 8)
     for t in range(4):
-        v.tensor_scalar(T.offs[:, 32 * t:32 * t + 32], T.quad[:], t, None, ADD).then_inc(S.voff, 1)
+        v.tensor_scalar(T.tab2[0:32, t:128:4], T.tab1[0:32, :], 4.0, float(t), MUL, ADD).then_inc(S.vt2, 1)
+    v.wait_ge(S.vt2, 4)
+    v.transpose(T.tab3[0:32, :], T.tab2[0:32, :]).then_inc(S.vt3, 1)
+    v.wait_ge(S.vt3, 1)
+    for k in range(4):
+        v.tensor_copy(T.offs[32 * k:32 * k + 32, :], T.tab3[0:32, :]).then_inc(S.voff, 1)
     for e in (v, a):
         e.wait_ge(S.voff, 4)
         e.wait_ge(S.lw1, 16)
+
+    def gather(lo, hi):
+        return T.ab[:, 4 * lo:4 * hi], T.w1b[:, 0:4096].indirect(T.offs[:, lo // 4:hi // 4])
+
     for k, (lo, hi) in enumerate(((0, 256), (256, 512))):
-
-        def gather(t):
-            return (T.ab[:, 4 * lo + t:4 * hi:4],
-                    T.w1b[:, 0:4096].indirect(T.offs[:, 32 * t + lo // 16:32 * t + hi // 16]))
-
-        for t in (0, 1):
-            v.tensor_copy(*gather(t)).then_inc(S["gath%d" % k], 1)
-        for t in (2, 3):
-            a.activation(*gather(t), COPY).then_inc(S["gath%d" % k], 1)
-        v.wait_ge(S["gath%d" % k], 4)
+        v.tensor_copy(*gather(lo, (lo + hi) // 2)).then_inc(S["gath%d" % k], 1)
+        a.activation(*gather((lo + hi) // 2, hi), COPY).then_inc(S["gath%d" % k], 1)
+        v.wait_ge(S["gath%d" % k], 2)
         v.quantize_mx(q("aq", r, lo, hi - lo), q("ap", r, lo, hi - lo), T.ab[:, 4 * lo:4 * hi]).then_inc(S["qa%d" % k], 1)
     v.wait_ge(S.lx, 16)
     v.wait_ge(S.lxg, 16)
@@ -139,40 +160,48 @@ def rank_program(g, core, T, topo):
         else:
             a.activation(out, z, RELU, scale=0.05).then_inc(S["e%d" % b], 1)
 
-    def hidden(i, scal, vect):
+    def pack(i):
         s = order[i]
-        for b in scal:
-            relu(i, b, False)
-        for b in vect:
-            relu(i, b, True)
         for b in range(4):
             v.wait_ge(S["e%d" % b], i + 1)
         v.quantize_mx(q("hq", s), q("hp", s), T["h%d" % s][:]).then_inc(S["h%d" % s], 1)
 
-    def rows(t):
-        return T.bb[:, t:W:4], T.w2g[:, C * t:C * t + C]
+    def hidden(i, scal, vect):
+        for b in scal:
+            relu(i, b, False)
+        for b in vect:
+            relu(i, b, True)
+        pack(i)
 
-    for t in (0, 1):
-        a.wait_ge(S["ix%d" % t], 16)
-        a.activation(*rows(t), COPY).then_inc(S.bcs, 1)
+    def rows(t, lo=0, hi=C):
+        return T.bb[:, 4 * lo + t:4 * hi:4], T.w2g[:, C * t + lo:C * t + hi]
+
+    a.wait_ge(S.ix0, 16)
+    a.activation(*rows(0), COPY).then_inc(S.bcs, 1)
     hidden(0, (0, 2), (1, 3))
-    a.wait_ge(S.ix2, 16)
-    a.activation(*rows(2), COPY).then_inc(S.bcs, 1)
+    for t in (1, 2):
+        v.wait_ge(S["ix%d" % t], 16)
+        v.tensor_copy(*rows(t)).then_inc(S.bcs, 1)
+    relu(1, 1, True)
     v.wait_ge(S.ix3, 16)
-    v.tensor_copy(*rows(3)).then_inc(S.bcv, 1)
+    v.tensor_copy(*rows(3, 0, 128)).then_inc(S.bcv, 1)
+    v.tensor_copy(*rows(3, 128, 256)).then_inc(S.bcw, 1)
     v.wait_ge(S.bcv, 1)
     v.wait_ge(S.bcs, 3)
-    v.quantize_mx(q("bq", r), q("bp", r), T.bb[:]).then_inc(S.qb, 1)
-    hidden(1, (0, 1, 2), (3,))
-    hidden(2, (0, 2), (1, 3))
-    hidden(3, (0, 1, 2), (3,))
-    for o in range(4):
-        cols = slice(C * o, C * o + C)
-        (a if o % 2 else v).wait_ge(S["yd%d" % o], 1)
-        if o % 2 == 0:
-            v.tensor_copy(T.yb[:, cols], T.yps[:, cols]).then_inc(S["yc%d" % o], 1)
+    v.quantize_mx(q("bq", r, 0, 128), q("bp", r, 0, 128), T.bb[:, 0:C]).then_inc(S.qb0, 1)
+    v.tensor_copy(*rows(3, 256, C)).then_inc(S.bcw, 1)
+    v.wait_ge(S.bcw, 2)
+    v.quantize_mx(q("bq", r, 128, 384), q("bp", r, 128, 384), T.bb[:, C:W]).then_inc(S.qb, 1)
+    hidden(1, (0, 2, 3), ())
+    hidden(2, (0, 1, 2), (3,))
+    hidden(3, (0, 2), (1, 3))
+    for k, (o, lo, hi, ps) in enumerate(parts):
+        cols = slice(C * o + lo, C * o + hi)
+        (a if k % 2 else v).wait_ge(S["yd%d" % k], 1)
+        if k % 2 == 0:
+            v.tensor_copy(T.yb[:, cols], ps).then_inc(S["yc%d" % k], 1)
         else:
-            a.activation(T.yb[:, cols], T.yps[:, cols], COPY).then_inc(S["yc%d" % o], 1)
+            a.activation(T.yb[:, cols], ps, COPY).then_inc(S["yc%d" % k], 1)
 
     p = g.tensor
 
@@ -180,29 +209,29 @@ def rank_program(g, core, T, topo):
         s = order[i]
         for k in ("qa0", "qa1", "qx") if s == r else ():
             p.wait_ge(S[k], 1)
-        for k in ("ax", "ay") if s != r else ():
-            p.wait_ge(S["%s%d" % (k, s)], len(recv[s]))
         for b in range(4):
-            if s != r and b == 3:
-                p.wait_ge(S["az%d" % s], len(recv[s]))
             if i:
+                p.wait_ge(*arrival("a", i, "P"))
+                p.wait_ge(*arrival("a", i, str(b)))
                 p.wait_ge(S["e%d" % b], i)
             p.matmul_mx(T.zps[:, C * b:C * b + C], q("aq", s, 128 * b, 128), q("ap", s, 128 * b, 128), T.xq[:], T.xp[:],
                         True, True).then_inc(S["z%d" % b], 1)
 
-    def second(i, o):
+    def second(i, k):
         s = order[i]
-        if o == 0:
-            p.wait_ge(S["h%d" % s], 1)
-        if s == r:
-            if o == 0:
-                p.wait_ge(S.qb, 1)
-        elif o != 2:
-            p.wait_ge(S["%s%d" % (("bx", "by", None, "bz")[o], s)], len(recv[s]))
-        m = p.matmul_mx(T.yps[:, C * o:C * o + C], q("bq", s, 128 * o, 128), q("bp", s, 128 * o, 128), q("hq", s), q("hp", s),
+        o, lo, hi, ps = parts[k]
+        p.wait_ge(S["h%d" % s], 1)
+        if i:
+            p.wait_ge(*arrival("b", i, "P"))
+            p.wait_ge(*arrival("b", i, str(o)))
+        else:
+            p.wait_ge(S.qb if o else S.qb0, 1)
+            if k == 4:
+                p.wait_ge(S.e0, N)
+        m = p.matmul_mx(ps, q("bq", s, 128 * o, 128), q("bp", s, 128 * o, 128), q("hq", s, lo, hi - lo), q("hp", s, lo, hi - lo),
                         i == 0, i == N - 1)
         if i == N - 1:
-            m.then_inc(S["yd%d" % o], 1)
+            m.then_inc(S["yd%d" % k], 1)
 
     first(0)
     first(1)
@@ -210,11 +239,13 @@ def rank_program(g, core, T, topo):
     second(0, 0)
     second(0, 1)
     first(3)
-    for i, o in ((0, 2), (0, 3), (1, 0), (2, 0), (1, 1), (1, 2), (1, 3), (3, 0), (2, 1), (3, 1), (2, 2), (3, 2), (2, 3), (3, 3)):
-        second(i, o)
+    for i, k in ((0, 2), (0, 3), (1, 0), (2, 0), (1, 1), (0, 4), (3, 0), (2, 1), (3, 1), (1, 2), (2, 2), (3, 2),
+                 (1, 3), (1, 4), (2, 3), (3, 3), (2, 4), (3, 4)):
+        second(i, k)
 
-    for o in range(4):
-        cols = slice(C * o, C * o + C)
-        g.sync.wait_ge(S["yc%d" % o], 1)
-        g.sync.dma_start(T.y[:, cols], T.yb[:, cols]).then_inc(S.stored, 16)
-    g.sync.wait_ge(S.stored, 64)
+    for k, (o, lo, hi, ps) in enumerate(parts):
+        cols = slice(C * o + lo, C * o + hi)
+        e = a if k == 3 else g.sync
+        e.wait_ge(S["yc%d" % k], 1)
+        e.dma_start(T.y[:, cols], T.yb[:, cols]).then_inc(S.stored, 16)
+    g.sync.wait_ge(S.stored, 80)

from concourse.bass import DstId, RemoteDMATransfer, IndirectOffsetOnAxis
from concourse.mybir import dt, AluOpType, ActivationFunctionType

N, C = 4, 512
W = 4 * C
BF, F8 = "bfloat16", "float8_e4m3fn_x4"
SCRATCH = {
    "lst": ("sbuf", [128, 4], "int32"),
    "tab0": ("sbuf", [128, 16], "int32"),
    "tab1": ("sbuf", [128, 32], "float32"),
    "tab2": ("sbuf", [128, 128], "float32"),
    "tab3": ("sbuf", [128, 128], "float32"),
    "offs": ("sbuf", [128, 128], "uint16"),
    "w1b": ("sbuf", [128, 4096], BF), "xb": ("sbuf", [128, W], BF), "ab": ("sbuf", [128, W], BF),
    "w2g": ("sbuf", [128, W], BF), "bb": ("sbuf", [128, W], BF),
    "h0": ("sbuf", [128, W], BF), "h1": ("sbuf", [128, W], BF), "h2": ("sbuf", [128, W], BF), "h3": ("sbuf", [128, W], BF),
    "xq": ("sbuf", [128, C], F8), "xp": ("sbuf", [128, C], "uint8"),
    "aq": ("sbuf", [128, N * C], F8), "ap": ("sbuf", [128, N * C], "uint8"),
    "bq": ("sbuf", [128, N * C], F8), "bp": ("sbuf", [128, N * C], "uint8"),
    "hq": ("sbuf", [128, N * C], F8), "hp": ("sbuf", [128, N * C], "uint8"),
    "yb": ("sbuf", [128, W], "float32"),
    "zps": ("psum", [128, W], "float32"),
    "yps": ("psum", [128, W], "float32"),
}

NEAR, FAR, OVER, PASS = 1, 2, 3, 4
A_CALLS = [(2, {NEAR: ["01"], FAR: ["01"]}),
           (3, {NEAR: ["P"], FAR: ["P"]}),
           (3, {NEAR: ["23"], FAR: ["23"]}),
           (4, {PASS: ["P"]}),
           (4, {PASS: ["0123"]})]
B_CALLS = [{k: [p] for k in (NEAR, FAR, OVER)} for p in ("0", "P", "12", "3")]

SEMAPHORES = (["lact", "ltab", "lw1", "lx", "lxg", "vt1", "vt2", "vt3", "voff", "gath0", "gath1", "qa0", "qa1", "qx", "qb",
               "qb0", "bcs", "bcv", "bcw", "sent", "stored", "yd4", "yc4"]
              + ["%s%d" % (k, i) for i in range(4) for k in ("ix", "z", "e", "h", "yd", "yc")]
              + ["a%d_%d" % (j, s) for j in range(len(A_CALLS)) for s in range(N)]
              + ["b%d_%d" % (j, s) for j in range(len(B_CALLS)) for s in range(N)])


def others(core, cores, topo):
    def kind(c):
        return 0 if c == core else NEAR if topo.chip(c) == topo.chip(core) else FAR if topo.die(c) == topo.die(core) else OVER
    return sorted(range(N), key=lambda s: kind(cores[s]))


def lanes(call, core, cores, topo):
    order = others(core, cores, topo)
    off = [(k, p) for k in (FAR, OVER) for p in call.get(k, [])]
    on = [(k, p) for k in (NEAR, PASS) for p in call.get(k, [])]
    out = topo.engines(core, cores[order[FAR]]) if off else []
    plan = {}
    for group, es in ((off, out), (on, [e for e in topo.engines(core, cores[order[NEAR]]) if e not in out])):
        n = [1] * len(group)
        while group and sum(n) + min(n) <= len(es):
            n[n.index(min(n))] *= 2
        for i, (k, p) in enumerate(group):
            plan.setdefault(k, []).append((p, es[sum(n[:i]):sum(n[:i + 1])]))
    return plan


def rank_program(g, core, T, topo):
    r = T.rank_of(core)
    if r is None:
        return
    S = T.sem
    MUL, ADD, MAX = AluOpType.mult, AluOpType.add, AluOpType.max
    COPY, RELU = ActivationFunctionType.Copy, ActivationFunctionType.Relu
    cores = list(T.cores)
    order = others(core, cores, topo)
    calls = {"a": [c for _, c in A_CALLS], "b": B_CALLS}

    def q(name, s, a=0, n=C):
        return T[name][:, C * s + a:C * s + a + n]

    def arrival(m, i, piece):
        for j, call in enumerate(calls[m]):
            for k, sender in ((i, order[i]), (PASS if i == OVER else None, order[NEAR])):
                if any(piece in p for p in call.get(k, [])):
                    return S["%s%d_%d" % (m, j, order[i])], sum(len(es) for _, es in lanes(call, cores[sender], cores, topo)[k])

    parts = [(o, 0, C, T.yps[:, C * o:C * o + C]) for o in range(3)]
    parts += [(3, 0, C // 2, T.yps[:, 3 * C:3 * C + C // 2]), (3, C // 2, C, T.zps[:, 0:C // 2])]

    XG = 256
    g.sync.dma_start(T.lst[:], T.act[:]).then_inc(S.lact, 16)
    g.scalar.dma_start(T.tab0[0:32, :], T.act[:]).then_inc(S.ltab, 16)
    g.scalar.dma_start(T.w1b[:], T.w1[:]).then_inc(S.lw1, 16)
    g.scalar.dma_start(T.xb[:, XG:], T.x[:, XG:]).then_inc(S.lx, 16)
    g.dma_start(T.xb[:, 0:XG], T.x[:, 0:XG]).then_inc(S.lxg, 16)

    total = [0]

    def fused(m, j):
        tr = []
        for k, pieces in lanes(calls[m][j], core, cores, topo).items():
            s = order[FAR] if k == PASS else r
            rid, pid, _ = topo.addr(cores[order[NEAR if k == PASS else k]])
            for p, es in pieces:
                if k == PASS:
                    for piece in p:
                        g.wait_ge(*arrival(m, FAR, piece))
                ap = q(m + "p", s) if p == "P" else q(m + "q", s, 128 * int(p[0]), 128 * len(p)).bitcast(dt.uint8)
                tr.append(RemoteDMATransfer(dst_ids=[DstId(rid=rid, pnc=pid)], dma_engine_mask=sum(1 << e for e in es),
                                            remote_sem=S["%s%d_%d" % (m, j, s)], src=ap, dst=ap))
                total[0] += len(es)
        g.remote_dma_fused(tr, local_sem=S.sent)

    g.wait_ge(S.lact, 16)
    for t in range(5):
        for j, (ahead, call) in enumerate(A_CALLS):
            if ahead == t:
                g.wait_ge(S.qa0, 1)
                if j:
                    g.wait_ge(S.qa1, 1)
                fused("a", j)
        if t < 4:
            g.indirect_dma_start(T.w2g[:, C * t:C * t + C], None, T.w2[:], IndirectOffsetOnAxis(ap=T.lst[:, t:t + 1], axis=0),
                                 bounds_check=1023).then_inc(S["ix%d" % t], 16)
    for j in range(len(B_CALLS)):
        if j < 2:
            g.wait_ge((S.qb0, S.qb)[j], 1)
        fused("b", j)
    g.wait_ge(S.sent, total[0])

    v, a = g.vector, g.scalar
    v.wait_ge(S.ltab, 16)
    for k in range(8):
        v.tensor_copy(T.tab1[0:32, 4 * k:4 * k + 4], T.tab0[0:32, k // 2:16:4]).then_inc(S.vt1, 1)
    v.wait_ge(S.vt1, 8)
    for t in range(4):
        v.tensor_scalar(T.tab2[0:32, t:128:4], T.tab1[0:32, :], 4.0, float(t), MUL, ADD).then_inc(S.vt2, 1)
    v.wait_ge(S.vt2, 4)
    v.transpose(T.tab3[0:32, :], T.tab2[0:32, :]).then_inc(S.vt3, 1)
    v.wait_ge(S.vt3, 1)
    for k in range(4):
        v.tensor_copy(T.offs[32 * k:32 * k + 32, :], T.tab3[0:32, :]).then_inc(S.voff, 1)
    for e in (v, a):
        e.wait_ge(S.voff, 4)
        e.wait_ge(S.lw1, 16)

    def gather(lo, hi):
        return T.ab[:, 4 * lo:4 * hi], T.w1b[:, 0:4096].indirect(T.offs[:, lo // 4:hi // 4])

    for k, (lo, hi) in enumerate(((0, 256), (256, 512))):
        v.tensor_copy(*gather(lo, (lo + hi) // 2)).then_inc(S["gath%d" % k], 1)
        a.activation(*gather((lo + hi) // 2, hi), COPY).then_inc(S["gath%d" % k], 1)
        v.wait_ge(S["gath%d" % k], 2)
        v.quantize_mx(q("aq", r, lo, hi - lo), q("ap", r, lo, hi - lo), T.ab[:, 4 * lo:4 * hi]).then_inc(S["qa%d" % k], 1)
    v.wait_ge(S.lx, 16)
    v.wait_ge(S.lxg, 16)
    v.quantize_mx(T.xq[:], T.xp[:], T.xb[:]).then_inc(S.qx, 1)

    def relu(i, b, vec):
        e = v if vec else a
        out, z = T["h%d" % order[i]][:, b:W:4], T.zps[:, C * b:C * b + C]
        e.wait_ge(S["z%d" % b], i + 1)
        if vec:
            v.tensor_scalar(out, z, 0.0, 0.05, MAX, MUL).then_inc(S["e%d" % b], 1)
        else:
            a.activation(out, z, RELU, scale=0.05).then_inc(S["e%d" % b], 1)

    def pack(i):
        s = order[i]
        for b in range(4):
            v.wait_ge(S["e%d" % b], i + 1)
        v.quantize_mx(q("hq", s), q("hp", s), T["h%d" % s][:]).then_inc(S["h%d" % s], 1)

    def hidden(i, scal, vect):
        for b in scal:
            relu(i, b, False)
        for b in vect:
            relu(i, b, True)
        pack(i)

    def rows(t, lo=0, hi=C):
        return T.bb[:, 4 * lo + t:4 * hi:4], T.w2g[:, C * t + lo:C * t + hi]

    a.wait_ge(S.ix0, 16)
    a.activation(*rows(0), COPY).then_inc(S.bcs, 1)
    hidden(0, (0, 2), (1, 3))
    for t in (1, 2):
        v.wait_ge(S["ix%d" % t], 16)
        v.tensor_copy(*rows(t)).then_inc(S.bcs, 1)
    relu(1, 1, True)
    v.wait_ge(S.ix3, 16)
    v.tensor_copy(*rows(3, 0, 128)).then_inc(S.bcv, 1)
    v.tensor_copy(*rows(3, 128, 256)).then_inc(S.bcw, 1)
    v.wait_ge(S.bcv, 1)
    v.wait_ge(S.bcs, 3)
    v.quantize_mx(q("bq", r, 0, 128), q("bp", r, 0, 128), T.bb[:, 0:C]).then_inc(S.qb0, 1)
    v.tensor_copy(*rows(3, 256, C)).then_inc(S.bcw, 1)
    v.wait_ge(S.bcw, 2)
    v.quantize_mx(q("bq", r, 128, 384), q("bp", r, 128, 384), T.bb[:, C:W]).then_inc(S.qb, 1)
    hidden(1, (0, 2, 3), ())
    hidden(2, (0, 1, 2), (3,))
    hidden(3, (0, 2), (1, 3))
    for k, (o, lo, hi, ps) in enumerate(parts):
        cols = slice(C * o + lo, C * o + hi)
        (a if k % 2 else v).wait_ge(S["yd%d" % k], 1)
        if k % 2 == 0:
            v.tensor_copy(T.yb[:, cols], ps).then_inc(S["yc%d" % k], 1)
        else:
            a.activation(T.yb[:, cols], ps, COPY).then_inc(S["yc%d" % k], 1)

    p = g.tensor

    def first(i):
        s = order[i]
        for k in ("qa0", "qa1", "qx") if s == r else ():
            p.wait_ge(S[k], 1)
        for b in range(4):
            if i:
                p.wait_ge(*arrival("a", i, "P"))
                p.wait_ge(*arrival("a", i, str(b)))
                p.wait_ge(S["e%d" % b], i)
            p.matmul_mx(T.zps[:, C * b:C * b + C], q("aq", s, 128 * b, 128), q("ap", s, 128 * b, 128), T.xq[:], T.xp[:],
                        True, True).then_inc(S["z%d" % b], 1)

    def second(i, k):
        s = order[i]
        o, lo, hi, ps = parts[k]
        p.wait_ge(S["h%d" % s], 1)
        if i:
            p.wait_ge(*arrival("b", i, "P"))
            p.wait_ge(*arrival("b", i, str(o)))
        else:
            p.wait_ge(S.qb if o else S.qb0, 1)
            if k == 4:
                p.wait_ge(S.e0, N)
        m = p.matmul_mx(ps, q("bq", s, 128 * o, 128), q("bp", s, 128 * o, 128), q("hq", s, lo, hi - lo), q("hp", s, lo, hi - lo),
                        i == 0, i == N - 1)
        if i == N - 1:
            m.then_inc(S["yd%d" % k], 1)

    first(0)
    first(1)
    first(2)
    second(0, 0)
    second(0, 1)
    first(3)
    for i, k in ((0, 2), (0, 3), (1, 0), (2, 0), (1, 1), (0, 4), (3, 0), (2, 1), (3, 1), (1, 2), (2, 2), (3, 2),
                 (1, 3), (1, 4), (2, 3), (3, 3), (2, 4), (3, 4)):
        second(i, k)

    for k, (o, lo, hi, ps) in enumerate(parts):
        cols = slice(C * o + lo, C * o + hi)
        e = a if k == 3 else g.sync
        e.wait_ge(S["yc%d" % k], 1)
        e.dma_start(T.y[:, cols], T.yb[:, cols]).then_inc(S.stored, 16)
    g.sync.wait_ge(S.stored, 80)
